import numpy as np
import ml_dtypes


def mxq(x, axis, fmt="e4m3"):
    dtype, down = {"e4m3": (ml_dtypes.float8_e4m3fn, 7), "e5m2": (ml_dtypes.float8_e5m2, 14)}[fmt]
    v = np.moveaxis(np.asarray(x, np.float32).astype(ml_dtypes.bfloat16).astype(np.float64), axis, -1)
    blocks = v.reshape(v.shape[:-1] + (-1, 32))
    amax = np.abs(blocks).max(-1, keepdims=True)
    byte = np.maximum(np.where(amax > 0, np.frexp(amax)[1] - 1 + 127, 0) - down, 1)
    scale = np.exp2(byte - 127.0)
    codes = (blocks / scale).astype(np.float32).astype(dtype).astype(np.float64)
    return np.moveaxis((codes * scale).reshape(v.shape), -1, axis)


WIDE = False


def mx_kscale(k):
    if not WIDE:
        return np.ones(k)
    levels = np.array([10, -10, 5, -5, 0])
    if k % 512:
        return np.exp2(np.random.permutation(np.resize(levels, k // 32))).repeat(32)
    a = np.empty((k // 512, 16))
    for p in range(k // 512):
        a[p, :8] = np.random.permutation(np.resize(levels, 8))
        for g in range(8):
            far = levels[np.abs(levels - a[p, g]) >= 10]
            a[p, g + 8] = far[np.random.randint(len(far))]
    return np.exp2(a.ravel()).repeat(32)


def f64(x):
    return np.asarray(x).astype(np.float64)


def striped(idx):
    return np.tile(idx.reshape(-1, 16).T, (8, 1)).astype(np.uint16)


def unstriped(offs):
    return offs[:16].T.reshape(-1).astype(np.int64)


K, T, E, C, N = 256, 1536, 24, 128, 512


def by_expert(wq, xq):
    return np.concatenate([wq[e].T @ xq[:, e * C:(e + 1) * C] for e in range(E)], axis=1)


def setup_inputs():
    n = np.random.standard_normal
    s = mx_kscale(N)[:, None]
    first = np.random.permutation(np.repeat(np.arange(E), T // E))
    second = (first + 1 + np.random.permutation(np.repeat(np.arange(E - 1), -(-T // (E - 1)))[:T])) % E
    while np.bincount(second, minlength=E).max() != T // E:
        load = np.bincount(second, minlength=E); hi, lo = int(load.argmax()), int(load.argmin())
        t = np.flatnonzero((second == hi) & (first != lo))[0]; second[t] = lo
    slot_token = np.empty(E * C, np.int64); pos = np.empty((2, T), np.int64); fill = np.zeros(E, np.int64)
    place = np.stack([np.random.permutation(C) for _ in range(E)])
    for r, deal in enumerate((first, second)):
        for t in np.random.permutation(T):
            e = deal[t]; j = e * C + place[e, fill[e]]; fill[e] += 1; slot_token[j] = t; pos[r, t] = j
    g = np.random.uniform(0.2, 0.8, T)
    w_slot = np.empty(E * C); w_slot[pos[0]] = g; w_slot[pos[1]] = 1.0 - g
    return {
        "dyT": (n((N, T)) * s).astype(np.float32),
        "w": (n((E, N, K)) / np.sqrt(N) / s[None]).astype(np.float32),
        "gate": np.tile(w_slot, (N, 1)).astype(np.float32),
        "offs": striped(slot_token),
        "pos1": striped(pos[0]),
        "pos2": striped(pos[1]),
    }


def reference(dyT, w, gate, offs, pos1, pos2):
    idx = unstriped(offs)
    gq = mxq(f64(gate) * f64(dyT)[:, idx], 0, "e4m3")
    dx = by_expert(mxq(f64(w), 1, "e4m3"), gq)
    return dx[:, unstriped(pos1)] + dx[:, unstriped(pos2)]

@@ -1,0 +1,182 @@
+import concourse.mybir as mybir
+
+N, K, T, E, C = 512, 256, 1536, 24, 128
+S = E * C
+FLOPS = 2 * N * K * S
+BYTES = 4 * (N * T + E * N * K + S + K * T) + 2 * (S + 2 * T)
+
+P = 128
+J = 4
+F32 = mybir.dt.float32
+BF16 = mybir.dt.bfloat16
+U32 = mybir.dt.uint32
+U16 = mybir.dt.uint16
+U8 = mybir.dt.uint8
+FP8X4 = mybir.dt.float8_e4m3fn_x4
+MULT = mybir.AluOpType.mult
+ADD = mybir.AluOpType.add
+
+PIECE = 512
+CHUNKS = [8, 8, 4, 4]
+FIN = [[768, 768], [768, 768]]
+RAWB, G4B, GGB, WGB = 9, 2, 2, 4
+ORDER = "offs d0 g0 d1 w0 d2 w1 d3 w2_3 g1 w4_5 w6_7 w8_9 pos w10_11 g2 w12_13 w14_15 g3 w16_17 w18_19 w20_21 w22_23"
+ON_VECTOR = {(11, 0), (11, 1), (11, 2), (15, 0), (15, 1), (15, 2), (19, 0), (19, 1), (19, 2), (23, 0), (23, 1), (23, 2), (3, 0), (3, 1), (3, 2), (7, 0), (7, 1), (7, 2)}
+ON_GPSIMD = {}
+PLAN = """
+G.0.0 G.0.1 W.0.2 G.0.2 W.1.2 QW.0.2 G.0.3 W.2.2 W.3.2 PG.0 G.1.0 W.4.2 QW.2.2 QG.0 W.5.2 G.1.1
+M.0.0 M.0.1 W.6.2 PG.1 QW.4.2 W.7.2 G.1.2 E.0.0 E.0.1 W.8.0 QW.6.2 W.9.0 QG.1 W.10.0 G.1.3 M.1.0
+M.1.1 E.1.0 E.1.1 W.12.0 W.11.0 W.13.0 G.2.0 W.14.0 PG.2 QW.8.0 W.15.0 G.2.1 PG.3 QW.12.0 QG.2 G.2.2
+M.2.0 E.2.0 QG.3 W.16.0 G.2.3 M.3.0 W.17.0 E.3.0 W.19.0 W.18.0 G.3.0 PG.4 QW.16.0 G.3.1 W.20.0 QG.4
+W.21.0 G.3.2 M.4.0 W.22.0 E.4.0 G.3.3 W.8.1 W.9.1 W.23.0 PG.5 W.11.1 QW.20.0 W.15.1 W.19.1 W.23.1
+W.10.1 QG.5 W.12.1 QW.8.1 M.5.0 W.13.1 M.2.1 E.5.0 E.2.1 C.1.0.0 W.14.1 W.16.1 QW.12.1 W.17.1 W.18.1
+C.2.0.0 M.3.1 W.20.1 E.3.1 QW.16.1 W.21.1 A.0.0 W.22.1 M.4.1 E.4.1 QW.20.1 S.0.0 C.1.0.1 M.5.1 E.5.1
+C.2.0.1 C.1.1.0 A.0.1 C.2.1.0 S.0.1 C.2.1.1 A.1.0 C.1.1.1 S.1.0 A.1.1 S.1.1
+"""
+
+
+def tile_moe_bdx_lin_none_kernel(tc, dyT, w, gate, offs, pos1, pos2, out):
+    nc = tc.nc
+    starts = [sum(CHUNKS[:c]) for c in range(len(CHUNKS))]
+    with (
+        tc.tile_pool(name="held", bufs=1) as held,
+        tc.tile_pool(name="stage", bufs=2) as stage,
+        tc.psum_pool(name="psum", bufs=8) as psum,
+    ):
+        lo = held.tile([P, S // 16], U16, name="lo")
+        l1 = held.tile([P, T // 16], U16, name="l1")
+        l2 = held.tile([P, T // 16], U16, name="l2")
+        dy = [held.tile([P, T], F32, name=f"dy{j}") for j in range(J)]
+        gates = [held.tile([P, C * n], F32, name=f"gate{c}") for c, n in enumerate(CHUNKS)]
+        dx = [held.tile([P, S], F32, name=f"dx{h}") for h in range(2)]
+        gcodes = [held.tile([P, PIECE], U32, name=f"gc{b}", align_bytes=64) for b in range(S // PIECE)]
+        gscales = [held.tile([P, PIECE], U8, name=f"gs{b}", align_bytes=64) for b in range(S // PIECE)]
+        planes = dyT.rearrange("(p j) t -> p j t", j=J)
+        raws = {}
+        g4 = {}
+        wg = {}
+        wc = {}
+        gg = {}
+        bank = {}
+        picked = {}
+
+        for item in ORDER.split():
+            if item == "offs":
+                nc.sync.dma_start(lo[:], offs)
+            elif item == "pos":
+                nc.sync.dma_start(l1[:], pos1)
+                nc.sync.dma_start(l2[:], pos2)
+            elif item.startswith("d"):
+                j = int(item[1:])
+                nc.sync.dma_start(out=dy[j][:], in_=planes[:, j, :])
+            elif item.startswith("g"):
+                c = int(item[1:])
+                a = starts[c] * C
+                nc.sync.dma_start(out=gates[c][:], in_=gate[0:P, a : a + CHUNKS[c] * C])
+            else:
+                es = [int(x) for x in item[1:].split("_")]
+                if es[0] // 2 not in raws:
+                    raws[es[0] // 2] = stage.tile([P, 2, J, K], F32, name="raw", bufs=RAWB)
+                x = es[0] % 2
+                nc.sync.dma_start(
+                    out=raws[es[0] // 2][:, x : x + len(es)].rearrange("p e j k -> p e (j k)"),
+                    in_=w[es[0] : es[0] + len(es)].rearrange("e (p j) k -> p e (j k)", j=J),
+                )
+
+        def group(on_vector, dst, source):
+            o = dst.rearrange("p (c i j) -> p c j i", i=4, j=J)
+            s = source.rearrange("p j (c i) -> p c j i", i=4)
+            if on_vector:
+                nc.vector.tensor_copy(out=o, in_=s)
+            else:
+                nc.scalar.copy(out=o, in_=s)
+
+        def gather(c, j):
+            a = starts[c] * C
+            n = CHUNKS[c] * C
+            if j == 0:
+                g4[c] = stage.tile([P, J, n], F32, name="g4", bufs=G4B)
+            nc.vector.tensor_tensor(
+                g4[c][:, j, :], dy[j][:].indirect(lo[:, a // 16 : (a + n) // 16]), gates[c][:], MULT
+            )
+
+        def pack_g(b):
+            c = [x for x in range(len(CHUNKS)) if starts[x] * C <= b * PIECE][-1]
+            at = b * PIECE - starts[c] * C
+            gg[b] = stage.tile([P, PIECE * J], BF16, name="gg", bufs=GGB, align_bytes=64)
+            group(("PG", b) in ON_VECTOR, gg[b][:], g4[c][:, :, at : at + PIECE])
+
+        def quant_g(b):
+            nc.vector.quantize_mx(out=gcodes[b][:].bitcast(FP8X4), scales=gscales[b][:], in_=gg[b][:])
+
+        def pack_w(e, h):
+            kw = P if h < 2 else 2 * P
+            per = PIECE // kw
+            key = (e // per, h)
+            if key not in wg:
+                wg[key] = stage.tile([P, PIECE * J], BF16, name="wg", bufs=WGB, align_bytes=64)
+            k0 = P if h == 1 else 0
+            at = e % per * kw * J
+            group((e, h) in ON_VECTOR, wg[key][:, at : at + kw * J], raws[e // 2][:, e % 2, :, k0 : k0 + kw])
+
+        def quant_w(first, h):
+            kw = P if h < 2 else 2 * P
+            per = PIECE // kw
+            codes = stage.tile([P, PIECE], U32, name="wc", bufs=6, align_bytes=64)
+            scales = stage.tile([P, PIECE], U8, name="ws", bufs=6, align_bytes=64)
+            nc.vector.quantize_mx(out=codes[:].bitcast(FP8X4), scales=scales[:], in_=wg[first // per, h][:])
+            for x in range(per):
+                if h < 2:
+                    wc[first + x, h] = (codes, scales, x * P)
+                else:
+                    wc[first + x, 0] = (codes, scales, 2 * x * P)
+                    wc[first + x, 1] = (codes, scales, (2 * x + 1) * P)
+
+        def multiply(b, h):
+            bank[b, h] = psum.tile([P, PIECE], F32, name="bank")
+            for x in range(PIECE // C):
+                codes, scales, at = wc[b * (PIECE // C) + x, h]
+                cols = slice(x * C, (x + 1) * C)
+                nc.tensor.matmul_mx(
+                    out=bank[b, h][:, cols],
+                    lhsT=codes[:, at : at + P].bitcast(FP8X4),
+                    lhsT_scale=scales[:, at : at + P],
+                    rhs=gcodes[b][:, cols].bitcast(FP8X4),
+                    rhs_scale=gscales[b][:, cols],
+                    start=True,
+                    stop=True,
+                )
+
+        def evict(b, h):
+            cols = slice(b * PIECE, (b + 1) * PIECE)
+            if ("E", b, h) in ON_VECTOR:
+                nc.vector.tensor_copy(out=dx[h][:, cols], in_=bank[b, h][:])
+            else:
+                nc.scalar.copy(out=dx[h][:, cols], in_=bank[b, h][:])
+
+        def span(h, q):
+            a = sum(FIN[h][:q])
+            return a, a + FIN[h][q]
+
+        def pick(which, h, q):
+            a, z = span(h, q)
+            t = stage.tile([P, z - a], F32, name=f"pick{which}", bufs=2)
+            nc.vector.tensor_copy(t[:], dx[h][:].indirect((l1 if which == 1 else l2)[:, a // 16 : z // 16]))
+            picked[which, h, q] = t
+
+        def add(h, q):
+            one, two = picked[1, h, q], picked[2, h, q]
+            engine = nc.gpsimd if ("ADD", h, q) in ON_GPSIMD else nc.vector
+            engine.tensor_tensor(out=one[:], in0=one[:], in1=two[:], op=ADD)
+
+        def store(h, q):
+            a, z = span(h, q)
+            nc.sync.dma_start(out=out[h * P : (h + 1) * P, a:z], in_=picked[1, h, q][:])
+
+        steps = {
+            "G": gather, "PG": pack_g, "QG": quant_g, "W": pack_w, "QW": quant_w, "M": multiply,
+            "E": evict, "C": pick, "A": add, "S": store,
+        }
+        for item in PLAN.split():
+            words = item.split(".")
+            steps[words[0]](*[int(x) for x in words[1:]])

@@ -17,21 +17,20 @@ MULT = mybir.AluOpType.mult
 ADD = mybir.AluOpType.add
 
 PIECE = 512
-CHUNKS = [8, 8, 4, 4]
+CHUNKS = [8, 8, 8]
 FIN = [[768, 768], [768, 768]]
+WHOLE = 8
 RAWB, G4B, GGB, WGB = 9, 2, 2, 4
-ORDER = "offs d0 g0 d1 w0 d2 w1 d3 w2_3 g1 w4_5 w6_7 w8_9 pos w10_11 g2 w12_13 w14_15 g3 w16_17 w18_19 w20_21 w22_23"
-ON_VECTOR = {(11, 0), (11, 1), (11, 2), (15, 0), (15, 1), (15, 2), (19, 0), (19, 1), (19, 2), (23, 0), (23, 1), (23, 2), (3, 0), (3, 1), (3, 2), (7, 0), (7, 1), (7, 2)}
-ON_GPSIMD = {}
+ORDER = "offs d0 g0 d1 d2 d3 u0 g1 u1 u2 u3 g2 u4 pos u5 u6 u7 u8 u9 u10 u11"
+ON_VECTOR = {('PG', 5), ('W', 10), ('W', 4), ('W', 6), ('W', 8)}
+ON_GPSIMD = {('A', 0, 0), ('A', 0, 1), ('A', 1, 0)}
 PLAN = """
-G.0.0 G.0.1 W.0.2 G.0.2 W.1.2 QW.0.2 G.0.3 W.2.2 W.3.2 PG.0 G.1.0 W.4.2 QW.2.2 QG.0 W.5.2 G.1.1
-M.0.0 M.0.1 W.6.2 PG.1 QW.4.2 W.7.2 G.1.2 E.0.0 E.0.1 W.8.0 QW.6.2 W.9.0 QG.1 W.10.0 G.1.3 M.1.0
-M.1.1 E.1.0 E.1.1 W.12.0 W.11.0 W.13.0 G.2.0 W.14.0 PG.2 QW.8.0 W.15.0 G.2.1 PG.3 QW.12.0 QG.2 G.2.2
-M.2.0 E.2.0 QG.3 W.16.0 G.2.3 M.3.0 W.17.0 E.3.0 W.19.0 W.18.0 G.3.0 PG.4 QW.16.0 G.3.1 W.20.0 QG.4
-W.21.0 G.3.2 M.4.0 W.22.0 E.4.0 G.3.3 W.8.1 W.9.1 W.23.0 PG.5 W.11.1 QW.20.0 W.15.1 W.19.1 W.23.1
-W.10.1 QG.5 W.12.1 QW.8.1 M.5.0 W.13.1 M.2.1 E.5.0 E.2.1 C.1.0.0 W.14.1 W.16.1 QW.12.1 W.17.1 W.18.1
-C.2.0.0 M.3.1 W.20.1 E.3.1 QW.16.1 W.21.1 A.0.0 W.22.1 M.4.1 E.4.1 QW.20.1 S.0.0 C.1.0.1 M.5.1 E.5.1
-C.2.0.1 C.1.1.0 A.0.1 C.2.1.0 S.0.1 C.2.1.1 A.1.0 C.1.1.1 S.1.0 A.1.1 S.1.1
+G.0.0 G.0.1 G.0.2 G.0.3 W.0 G.1.0 PG.0 QW.0 G.1.1 W.1 QG.0 G.1.2 W.2 QW.1 G.1.3 W.3 M.0.0 M.0.1 QW.2
+W.4 PG.1 QW.3 QW.4 E.0.0 QG.1 E.0.1 G.2.0 M.1.0 PG.2 M.1.1 G.2.1 E.1.0 E.1.1 W.5 QG.2 G.2.2 M.2.0
+PG.3 G.2.3 QW.5 E.2.0 QG.3 W.7 W.6 M.3.0 PG.5 E.3.0 QW.6 PG.4 QW.7 QG.5 W.8 M.5.0 E.5.0 QG.4 W.9
+QW.8 M.4.0 W.10 M.2.1 QW.10 E.4.0 QW.9 E.2.1 M.4.1 C.1.0.0 W.11 M.3.1 C.2.0.0 E.3.1 QW.11 A.0.0
+E.4.1 C.1.0.1 M.5.1 E.5.1 C.2.0.1 S.0.0 C.2.1.0 A.0.1 C.1.1.0 S.0.1 C.2.1.1 A.1.0 C.1.1.1 S.1.0
+A.1.1 S.1.1
 """
 
 
@@ -74,13 +73,11 @@ def tile_moe_bdx_lin_none_kernel(tc, dyT, w, gate, offs, pos1, pos2, out):
                 a = starts[c] * C
                 nc.sync.dma_start(out=gates[c][:], in_=gate[0:P, a : a + CHUNKS[c] * C])
             else:
-                es = [int(x) for x in item[1:].split("_")]
-                if es[0] // 2 not in raws:
-                    raws[es[0] // 2] = stage.tile([P, 2, J, K], F32, name="raw", bufs=RAWB)
-                x = es[0] % 2
+                u = int(item[1:])
+                raws[u] = stage.tile([P, 2, J, K], F32, name="raw", bufs=RAWB)
                 nc.sync.dma_start(
-                    out=raws[es[0] // 2][:, x : x + len(es)].rearrange("p e j k -> p e (j k)"),
-                    in_=w[es[0] : es[0] + len(es)].rearrange("e (p j) k -> p e (j k)", j=J),
+                    out=raws[u][:].rearrange("p e j k -> p e (j k)"),
+                    in_=w[2 * u : 2 * u + 2].rearrange("e (p j) k -> p e (j k)", j=J),
                 )
 
         def group(on_vector, dst, source):
@@ -109,28 +106,34 @@ def tile_moe_bdx_lin_none_kernel(tc, dyT, w, gate, offs, pos1, pos2, out):
         def quant_g(b):
             nc.vector.quantize_mx(out=gcodes[b][:].bitcast(FP8X4), scales=gscales[b][:], in_=gg[b][:])
 
-        def pack_w(e, h):
-            kw = P if h < 2 else 2 * P
-            per = PIECE // kw
-            key = (e // per, h)
-            if key not in wg:
-                wg[key] = stage.tile([P, PIECE * J], BF16, name="wg", bufs=WGB, align_bytes=64)
-            k0 = P if h == 1 else 0
-            at = e % per * kw * J
-            group((e, h) in ON_VECTOR, wg[key][:, at : at + kw * J], raws[e // 2][:, e % 2, :, k0 : k0 + kw])
+        units = [((e, e + 1), (0, 1)) for e in range(0, WHOLE, 2)]
+        units += [((e, e + 1, e + 2, e + 3), (h,)) for h in (0, 1) for e in range(WHOLE, E, 4)]
 
-        def quant_w(first, h):
-            kw = P if h < 2 else 2 * P
-            per = PIECE // kw
+        def pack_w(u):
+            experts, halves = units[u]
+            kw = P * len(halves)
+            k0 = P * halves[0]
+            wg[u] = stage.tile([P, PIECE * J], BF16, name="wg", bufs=WGB, align_bytes=64)
+            if ("W", u) in ON_VECTOR:
+                for x in range(0, len(experts), 2):
+                    nc.vector.tensor_copy(
+                        out=wg[u][:, x * kw * J : (x + 2) * kw * J].rearrange("p (e c i j) -> p e c j i", e=2, i=4, j=J),
+                        in_=raws[experts[x] // 2][:, :, :, k0 : k0 + kw].rearrange("p e j (c i) -> p e c j i", i=4),
+                    )
+            else:
+                for x, e in enumerate(experts):
+                    group(False, wg[u][:, x * kw * J : (x + 1) * kw * J], raws[e // 2][:, e % 2, :, k0 : k0 + kw])
+
+        def quant_w(u):
+            experts, halves = units[u]
             codes = stage.tile([P, PIECE], U32, name="wc", bufs=6, align_bytes=64)
             scales = stage.tile([P, PIECE], U8, name="ws", bufs=6, align_bytes=64)
-            nc.vector.quantize_mx(out=codes[:].bitcast(FP8X4), scales=scales[:], in_=wg[first // per, h][:])
-            for x in range(per):
-                if h < 2:
-                    wc[first + x, h] = (codes, scales, x * P)
-                else:
-                    wc[first + x, 0] = (codes, scales, 2 * x * P)
-                    wc[first + x, 1] = (codes, scales, (2 * x + 1) * P)
+            nc.vector.quantize_mx(out=codes[:].bitcast(FP8X4), scales=scales[:], in_=wg[u][:])
+            at = 0
+            for e in experts:
+                for h in halves:
+                    wc[e, h] = (codes, scales, at)
+                    at += P
 
         def multiply(b, h):
             bank[b, h] = psum.tile([P, PIECE], F32, name="bank")
@@ -166,7 +169,7 @@ def tile_moe_bdx_lin_none_kernel(tc, dyT, w, gate, offs, pos1, pos2, out):
 
         def add(h, q):
             one, two = picked[1, h, q], picked[2, h, q]
-            engine = nc.gpsimd if ("ADD", h, q) in ON_GPSIMD else nc.vector
+            engine = nc.gpsimd if ("A", h, q) in ON_GPSIMD else nc.vector
             engine.tensor_tensor(out=one[:], in0=one[:], in1=two[:], op=ADD)
 
         def store(h, q):

@@ -19,18 +19,21 @@ ADD = mybir.AluOpType.add
 PIECE = 512
 CHUNKS = [8, 8, 8]
 FIN = [[768, 768], [768, 768]]
-WHOLE = 8
-RAWB, G4B, GGB, WGB = 9, 2, 2, 4
-ORDER = "offs d0 g0 d1 d2 d3 u0 g1 u1 u2 u3 g2 u4 pos u5 u6 u7 u8 u9 u10 u11"
-ON_VECTOR = {('PG', 5), ('W', 10), ('W', 4), ('W', 6), ('W', 8)}
+UNITS = [((0, 1), (0, 1)), ((2, 3), (0, 1)), ((4, 5, 6, 7), (0, 1)), ((8, 9, 10, 11), (0,)), ((12, 13, 14, 15), (0,)), ((16, 17, 18, 19), (0,)), ((20, 21, 22, 23), (0,)), ((8, 9, 10, 11), (1,)), ((12, 13, 14, 15), (1,)), ((16, 17, 18, 19), (1,)), ((20, 21, 22, 23), (1,))]
+RAWB, G4B, GGB = 8, 2, 2
+WGB = {512: 4, 1024: 1}
+WCB = {512: 5, 1024: 1}
+ORDER = "offs d0 g0 d1 d2 s0 d3 s1 g1 u1 u2 u3 u4 pos g2 u5 u6 u7 u8 u9 u10 u11"
+ON_VECTOR = {('W', 10), ('W', 3), ('W', 5), ('W', 6), ('W', 7)}
 ON_GPSIMD = {('A', 0, 0), ('A', 0, 1), ('A', 1, 0)}
 PLAN = """
-G.0.0 G.0.1 G.0.2 G.0.3 W.0 G.1.0 PG.0 QW.0 G.1.1 W.1 QG.0 G.1.2 W.2 QW.1 G.1.3 W.3 M.0.0 M.0.1 QW.2
-W.4 PG.1 QW.3 QW.4 E.0.0 QG.1 E.0.1 G.2.0 M.1.0 PG.2 M.1.1 G.2.1 E.1.0 E.1.1 W.5 QG.2 G.2.2 M.2.0
-PG.3 G.2.3 QW.5 E.2.0 QG.3 W.7 W.6 M.3.0 PG.5 E.3.0 QW.6 PG.4 QW.7 QG.5 W.8 M.5.0 E.5.0 QG.4 W.9
-QW.8 M.4.0 W.10 M.2.1 QW.10 E.4.0 QW.9 E.2.1 M.4.1 C.1.0.0 W.11 M.3.1 C.2.0.0 E.3.1 QW.11 A.0.0
-E.4.1 C.1.0.1 M.5.1 E.5.1 C.2.0.1 S.0.0 C.2.1.0 A.0.1 C.1.1.0 S.0.1 C.2.1.1 A.1.0 C.1.1.1 S.1.0
-A.1.1 S.1.1
+G.0.0 G.0.1 W.0.0 G.0.2 G.0.3 W.0.1 QW.0 PG.0 G.1.0 W.1.0 G.1.1 W.1.1 QG.0 W.2.0 G.1.2 W.2.1 QW.1
+W.2.2 G.1.3 M.0.0 M.0.1 W.2.3 W.3.0 PG.1 W.3.1 QW.2 QW.3 E.0.0 QG.1 E.0.1 G.2.0 M.1.0 W.4.0 M.1.1
+E.1.0 E.1.1 G.2.1 W.4.1 W.4.2 W.4.3 G.2.2 PG.2 QW.4 G.2.3 PG.3 QG.2 W.5.0 M.2.0 PG.4 QG.3 W.5.1
+M.3.0 W.6.0 QW.5 E.2.0 W.6.1 E.3.0 QG.4 PG.5 QW.6 M.4.0 W.7.0 W.7.1 W.10.0 E.4.0 QG.5 W.8.0 QW.7
+M.5.0 W.8.1 W.10.1 M.2.1 E.5.0 QW.10 E.2.1 C.1.0.0 W.8.2 M.5.1 W.8.3 C.2.0.0 W.9.0 W.9.1 W.9.2 QW.8
+A.0.0 C.1.0.1 W.9.3 M.3.1 E.3.1 S.0.0 E.5.1 QW.9 C.2.0.1 M.4.1 E.4.1 C.2.1.0 A.0.1 C.1.1.0 S.0.1
+C.2.1.1 A.1.0 S.1.0 C.1.1.1 A.1.1 S.1.1
 """
 
 
@@ -73,11 +76,13 @@ def tile_moe_bdx_lin_none_kernel(tc, dyT, w, gate, offs, pos1, pos2, out):
                 a = starts[c] * C
                 nc.sync.dma_start(out=gates[c][:], in_=gate[0:P, a : a + CHUNKS[c] * C])
             else:
-                u = int(item[1:])
-                raws[u] = stage.tile([P, 2, J, K], F32, name="raw", bufs=RAWB)
+                first, count = (int(item[1:]), 1) if item.startswith("s") else (2 * int(item[1:]), 2)
+                u, x = first // 2, first % 2
+                if u not in raws:
+                    raws[u] = stage.tile([P, 2, J, K], F32, name="raw", bufs=RAWB)
                 nc.sync.dma_start(
-                    out=raws[u][:].rearrange("p e j k -> p e (j k)"),
-                    in_=w[2 * u : 2 * u + 2].rearrange("e (p j) k -> p e (j k)", j=J),
+                    out=raws[u][:, x : x + count].rearrange("p e j k -> p e (j k)"),
+                    in_=w[first : first + count].rearrange("e (p j) k -> p e (j k)", j=J),
                 )
 
         def group(on_vector, dst, source):
@@ -106,28 +111,33 @@ def tile_moe_bdx_lin_none_kernel(tc, dyT, w, gate, offs, pos1, pos2, out):
         def quant_g(b):
             nc.vector.quantize_mx(out=gcodes[b][:].bitcast(FP8X4), scales=gscales[b][:], in_=gg[b][:])
 
-        units = [((e, e + 1), (0, 1)) for e in range(0, WHOLE, 2)]
-        units += [((e, e + 1, e + 2, e + 3), (h,)) for h in (0, 1) for e in range(WHOLE, E, 4)]
-
-        def pack_w(u):
-            experts, halves = units[u]
+        def pack_w(u, x):
+            experts, halves = UNITS[u]
             kw = P * len(halves)
             k0 = P * halves[0]
-            wg[u] = stage.tile([P, PIECE * J], BF16, name="wg", bufs=WGB, align_bytes=64)
+            if u not in wg:
+                width = kw * len(experts)
+                wg[u] = stage.tile([P, width * J], BF16, name=f"wg{width}", bufs=WGB[width], align_bytes=64)
             if ("W", u) in ON_VECTOR:
-                for x in range(0, len(experts), 2):
-                    nc.vector.tensor_copy(
-                        out=wg[u][:, x * kw * J : (x + 2) * kw * J].rearrange("p (e c i j) -> p e c j i", e=2, i=4, j=J),
-                        in_=raws[experts[x] // 2][:, :, :, k0 : k0 + kw].rearrange("p e j (c i) -> p e c j i", i=4),
-                    )
+                e = experts[2 * x]
+                nc.vector.tensor_copy(
+                    out=wg[u][:, 2 * x * kw * J : (2 * x + 2) * kw * J].rearrange("p (e c i j) -> p e c j i", e=2, i=4, j=J),
+                    in_=raws[e // 2][:, :, :, k0 : k0 + kw].rearrange("p e j (c i) -> p e c j i", i=4),
+                )
             else:
-                for x, e in enumerate(experts):
-                    group(False, wg[u][:, x * kw * J : (x + 1) * kw * J], raws[e // 2][:, e % 2, :, k0 : k0 + kw])
+                e = experts[x]
+                dst = wg[u][:, x * kw * J : (x + 1) * kw * J].rearrange("p (c i j) -> p c j i", i=4, j=J)
+                source = raws[e // 2][:, e % 2, :, k0 : k0 + kw].rearrange("p j (c i) -> p c j i", i=4)
+                if ("W", u) in ON_GPSIMD:
+                    nc.gpsimd.tensor_scalar(out=dst, in0=source, scalar1=1.0, scalar2=0.0, op0=MULT, op1=ADD)
+                else:
+                    nc.scalar.copy(out=dst, in_=source)
 
         def quant_w(u):
-            experts, halves = units[u]
-            codes = stage.tile([P, PIECE], U32, name="wc", bufs=6, align_bytes=64)
-            scales = stage.tile([P, PIECE], U8, name="ws", bufs=6, align_bytes=64)
+            experts, halves = UNITS[u]
+            width = P * len(halves) * len(experts)
+            codes = stage.tile([P, width], U32, name=f"wc{width}", bufs=WCB[width], align_bytes=64)
+            scales = stage.tile([P, width], U8, name=f"ws{width}", bufs=WCB[width], align_bytes=64)
             nc.vector.quantize_mx(out=codes[:].bitcast(FP8X4), scales=scales[:], in_=wg[u][:])
             at = 0
             for e in experts:
@@ -163,7 +173,7 @@ def tile_moe_bdx_lin_none_kernel(tc, dyT, w, gate, offs, pos1, pos2, out):
 
         def pick(which, h, q):
             a, z = span(h, q)
-            t = stage.tile([P, z - a], F32, name=f"pick{which}", bufs=2)
+            t = stage.tile([P, z - a], F32, name=f"pick{which}", bufs=3)
             nc.vector.tensor_copy(t[:], dx[h][:].indirect((l1 if which == 1 else l2)[:, a // 16 : z // 16]))
             picked[which, h, q] = t
 

import concourse.mybir as mybir

N, K, T, E, C = 512, 256, 1536, 24, 128
S = E * C
FLOPS = 2 * N * K * S
BYTES = 4 * (N * T + E * N * K + S + K * T) + 2 * (S + 2 * T)

P = 128
J = 4
F32 = mybir.dt.float32
BF16 = mybir.dt.bfloat16
U32 = mybir.dt.uint32
U16 = mybir.dt.uint16
U8 = mybir.dt.uint8
FP8X4 = mybir.dt.float8_e4m3fn_x4
MULT = mybir.AluOpType.mult
ADD = mybir.AluOpType.add

PIECE = 512
CHUNKS = [8, 8, 8]
FIN = [[768, 768], [768, 768]]
UNITS = [((0, 1), (0, 1)), ((2, 3), (0, 1)), ((4, 5, 6, 7), (0, 1)), ((8, 9, 10, 11), (0,)), ((12, 13, 14, 15), (0,)), ((16, 17, 18, 19), (0,)), ((20, 21, 22, 23), (0,)), ((8, 9, 10, 11), (1,)), ((12, 13, 14, 15), (1,)), ((16, 17, 18, 19), (1,)), ((20, 21, 22, 23), (1,))]
RAWB, G4B, GGB = 8, 2, 2
WGB = {512: 4, 1024: 1}
WCB = {512: 5, 1024: 1}
ORDER = "offs d0 g0 d1 d2 s0 d3 s1 g1 u1 u2 u3 u4 pos g2 u5 u6 u7 u8 u9 u10 u11"
ON_VECTOR = {('W', 10), ('W', 3), ('W', 5), ('W', 6), ('W', 7)}
ON_GPSIMD = {('A', 0, 0), ('A', 0, 1), ('A', 1, 0)}
PLAN = """
G.0.0 G.0.1 W.0.0 G.0.2 G.0.3 W.0.1 QW.0 PG.0 G.1.0 W.1.0 G.1.1 W.1.1 QG.0 W.2.0 G.1.2 W.2.1 QW.1
W.2.2 G.1.3 M.0.0 M.0.1 W.2.3 W.3.0 PG.1 W.3.1 QW.2 QW.3 E.0.0 QG.1 E.0.1 G.2.0 M.1.0 W.4.0 M.1.1
E.1.0 E.1.1 G.2.1 W.4.1 W.4.2 W.4.3 G.2.2 PG.2 QW.4 G.2.3 PG.3 QG.2 W.5.0 M.2.0 PG.4 QG.3 W.5.1
M.3.0 W.6.0 QW.5 E.2.0 W.6.1 E.3.0 QG.4 PG.5 QW.6 M.4.0 W.7.0 W.7.1 W.10.0 E.4.0 QG.5 W.8.0 QW.7
M.5.0 W.8.1 W.10.1 M.2.1 E.5.0 QW.10 E.2.1 C.1.0.0 W.8.2 M.5.1 W.8.3 C.2.0.0 W.9.0 W.9.1 W.9.2 QW.8
A.0.0 C.1.0.1 W.9.3 M.3.1 E.3.1 S.0.0 E.5.1 QW.9 C.2.0.1 M.4.1 E.4.1 C.2.1.0 A.0.1 C.1.1.0 S.0.1
C.2.1.1 A.1.0 S.1.0 C.1.1.1 A.1.1 S.1.1
"""


def tile_moe_bdx_lin_none_kernel(tc, dyT, w, gate, offs, pos1, pos2, out):
    nc = tc.nc
    starts = [sum(CHUNKS[:c]) for c in range(len(CHUNKS))]
    with (
        tc.tile_pool(name="held", bufs=1) as held,
        tc.tile_pool(name="stage", bufs=2) as stage,
        tc.psum_pool(name="psum", bufs=8) as psum,
    ):
        lo = held.tile([P, S // 16], U16, name="lo")
        l1 = held.tile([P, T // 16], U16, name="l1")
        l2 = held.tile([P, T // 16], U16, name="l2")
        dy = [held.tile([P, T], F32, name=f"dy{j}") for j in range(J)]
        gates = [held.tile([P, C * n], F32, name=f"gate{c}") for c, n in enumerate(CHUNKS)]
        dx = [held.tile([P, S], F32, name=f"dx{h}") for h in range(2)]
        gcodes = [held.tile([P, PIECE], U32, name=f"gc{b}", align_bytes=64) for b in range(S // PIECE)]
        gscales = [held.tile([P, PIECE], U8, name=f"gs{b}", align_bytes=64) for b in range(S // PIECE)]
        planes = dyT.rearrange("(p j) t -> p j t", j=J)
        raws = {}
        g4 = {}
        wg = {}
        wc = {}
        gg = {}
        bank = {}
        picked = {}

        for item in ORDER.split():
            if item == "offs":
                nc.sync.dma_start(lo[:], offs)
            elif item == "pos":
                nc.sync.dma_start(l1[:], pos1)
                nc.sync.dma_start(l2[:], pos2)
            elif item.startswith("d"):
                j = int(item[1:])
                nc.sync.dma_start(out=dy[j][:], in_=planes[:, j, :])
            elif item.startswith("g"):
                c = int(item[1:])
                a = starts[c] * C
                nc.sync.dma_start(out=gates[c][:], in_=gate[0:P, a : a + CHUNKS[c] * C])
            else:
                first, count = (int(item[1:]), 1) if item.startswith("s") else (2 * int(item[1:]), 2)
                u, x = first // 2, first % 2
                if u not in raws:
                    raws[u] = stage.tile([P, 2, J, K], F32, name="raw", bufs=RAWB)
                nc.sync.dma_start(
                    out=raws[u][:, x : x + count].rearrange("p e j k -> p e (j k)"),
                    in_=w[first : first + count].rearrange("e (p j) k -> p e (j k)", j=J),
                )

        def group(on_vector, dst, source):
            o = dst.rearrange("p (c i j) -> p c j i", i=4, j=J)
            s = source.rearrange("p j (c i) -> p c j i", i=4)
            if on_vector:
                nc.vector.tensor_copy(out=o, in_=s)
            else:
                nc.scalar.copy(out=o, in_=s)

        def gather(c, j):
            a = starts[c] * C
            n = CHUNKS[c] * C
            if j == 0:
                g4[c] = stage.tile([P, J, n], F32, name="g4", bufs=G4B)
            nc.vector.tensor_tensor(
                g4[c][:, j, :], dy[j][:].indirect(lo[:, a // 16 : (a + n) // 16]), gates[c][:], MULT
            )

        def pack_g(b):
            c = [x for x in range(len(CHUNKS)) if starts[x] * C <= b * PIECE][-1]
            at = b * PIECE - starts[c] * C
            gg[b] = stage.tile([P, PIECE * J], BF16, name="gg", bufs=GGB, align_bytes=64)
            group(("PG", b) in ON_VECTOR, gg[b][:], g4[c][:, :, at : at + PIECE])

        def quant_g(b):
            nc.vector.quantize_mx(out=gcodes[b][:].bitcast(FP8X4), scales=gscales[b][:], in_=gg[b][:])

        def pack_w(u, x):
            experts, halves = UNITS[u]
            kw = P * len(halves)
            k0 = P * halves[0]
            if u not in wg:
                width = kw * len(experts)
                wg[u] = stage.tile([P, width * J], BF16, name=f"wg{width}", bufs=WGB[width], align_bytes=64)
            if ("W", u) in ON_VECTOR:
                e = experts[2 * x]
                nc.vector.tensor_copy(
                    out=wg[u][:, 2 * x * kw * J : (2 * x + 2) * kw * J].rearrange("p (e c i j) -> p e c j i", e=2, i=4, j=J),
                    in_=raws[e // 2][:, :, :, k0 : k0 + kw].rearrange("p e j (c i) -> p e c j i", i=4),
                )
            else:
                e = experts[x]
                dst = wg[u][:, x * kw * J : (x + 1) * kw * J].rearrange("p (c i j) -> p c j i", i=4, j=J)
                source = raws[e // 2][:, e % 2, :, k0 : k0 + kw].rearrange("p j (c i) -> p c j i", i=4)
                if ("W", u) in ON_GPSIMD:
                    nc.gpsimd.tensor_scalar(out=dst, in0=source, scalar1=1.0, scalar2=0.0, op0=MULT, op1=ADD)
                else:
                    nc.scalar.copy(out=dst, in_=source)

        def quant_w(u):
            experts, halves = UNITS[u]
            width = P * len(halves) * len(experts)
            codes = stage.tile([P, width], U32, name=f"wc{width}", bufs=WCB[width], align_bytes=64)
            scales = stage.tile([P, width], U8, name=f"ws{width}", bufs=WCB[width], align_bytes=64)
            nc.vector.quantize_mx(out=codes[:].bitcast(FP8X4), scales=scales[:], in_=wg[u][:])
            at = 0
            for e in experts:
                for h in halves:
                    wc[e, h] = (codes, scales, at)
                    at += P

        def multiply(b, h):
            bank[b, h] = psum.tile([P, PIECE], F32, name="bank")
            for x in range(PIECE // C):
                codes, scales, at = wc[b * (PIECE // C) + x, h]
                cols = slice(x * C, (x + 1) * C)
                nc.tensor.matmul_mx(
                    out=bank[b, h][:, cols],
                    lhsT=codes[:, at : at + P].bitcast(FP8X4),
                    lhsT_scale=scales[:, at : at + P],
                    rhs=gcodes[b][:, cols].bitcast(FP8X4),
                    rhs_scale=gscales[b][:, cols],
                    start=True,
                    stop=True,
                )

        def evict(b, h):
            cols = slice(b * PIECE, (b + 1) * PIECE)
            if ("E", b, h) in ON_VECTOR:
                nc.vector.tensor_copy(out=dx[h][:, cols], in_=bank[b, h][:])
            else:
                nc.scalar.copy(out=dx[h][:, cols], in_=bank[b, h][:])

        def span(h, q):
            a = sum(FIN[h][:q])
            return a, a + FIN[h][q]

        def pick(which, h, q):
            a, z = span(h, q)
            t = stage.tile([P, z - a], F32, name=f"pick{which}", bufs=3)
            nc.vector.tensor_copy(t[:], dx[h][:].indirect((l1 if which == 1 else l2)[:, a // 16 : z // 16]))
            picked[which, h, q] = t

        def add(h, q):
            one, two = picked[1, h, q], picked[2, h, q]
            engine = nc.gpsimd if ("A", h, q) in ON_GPSIMD else nc.vector
            engine.tensor_tensor(out=one[:], in0=one[:], in1=two[:], op=ADD)

        def store(h, q):
            a, z = span(h, q)
            nc.sync.dma_start(out=out[h * P : (h + 1) * P, a:z], in_=picked[1, h, q][:])

        steps = {
            "G": gather, "PG": pack_g, "QG": quant_g, "W": pack_w, "QW": quant_w, "M": multiply,
            "E": evict, "C": pick, "A": add, "S": store,
        }
        for item in PLAN.split():
            words = item.split(".")
            steps[words[0]](*[int(x) for x in words[1:]])
